import numpy as np
import ml_dtypes


def mxq(x, axis, fmt="e4m3"):
    dtype, down = {"e4m3": (ml_dtypes.float8_e4m3fn, 7), "e5m2": (ml_dtypes.float8_e5m2, 14)}[fmt]
    v = np.moveaxis(np.asarray(x, np.float32).astype(ml_dtypes.bfloat16).astype(np.float64), axis, -1)
    blocks = v.reshape(v.shape[:-1] + (-1, 32))
    amax = np.abs(blocks).max(-1, keepdims=True)
    byte = np.maximum(np.where(amax > 0, np.frexp(amax)[1] - 1 + 127, 0) - down, 1)
    scale = np.exp2(byte - 127.0)
    codes = (blocks / scale).astype(np.float32).astype(dtype).astype(np.float64)
    return np.moveaxis((codes * scale).reshape(v.shape), -1, axis)


WIDE = False


def mx_kscale(k):
    if not WIDE:
        return np.ones(k)
    levels = np.array([10, -10, 5, -5, 0])
    if k % 512:
        return np.exp2(np.random.permutation(np.resize(levels, k // 32))).repeat(32)
    a = np.empty((k // 512, 16))
    for p in range(k // 512):
        a[p, :8] = np.random.permutation(np.resize(levels, 8))
        for g in range(8):
            far = levels[np.abs(levels - a[p, g]) >= 10]
            a[p, g + 8] = far[np.random.randint(len(far))]
    return np.exp2(a.ravel()).repeat(32)


BF16 = ml_dtypes.bfloat16


def bf(x):
    return np.asarray(x, np.float32).astype(BF16)


def f64(x):
    return np.asarray(x).astype(np.float64)


V, K, U, E, B, T = 2048, 1024, 128, 8, 512, 8


def setup_inputs():
    s, t = mx_kscale(K), mx_kscale(V)
    topics = np.random.standard_normal((T, K))
    embed = np.repeat(topics, V // T, axis=0) + np.random.standard_normal((V, K))
    embed = embed / np.sqrt((embed * embed).sum(axis=1, keepdims=True))
    query = np.repeat(topics, U // T, axis=0) + 0.7 * np.random.standard_normal((U, K))
    centers = query[:, None, :] + 0.7 * np.random.standard_normal((U, E, K))
    centers = centers / np.sqrt((centers * centers).sum(axis=2, keepdims=True))
    sharp = np.linspace(1.0, 5.0, E)
    centers = (centers * sharp[:, None]).reshape(U * E, K).T
    affinity = np.repeat(np.random.standard_normal((T, B)), V // T, axis=0)
    counts = np.exp(0.8 * affinity + 0.5 * np.random.standard_normal((V, B))) / V
    return {"embed": bf(embed * s),
            "centers": bf(centers / s[:, None]),
            "idf": bf(np.exp(0.5 * np.random.standard_normal(V)) * t),
            "counts": bf(counts / t[:, None])}


def reference(embed, centers, idf, counts):
    cos = mxq(f64(embed), 1, "e4m3") @ mxq(f64(centers), 0, "e4m3")
    h = np.exp(cos) * f64(idf)[:, None]
    pooled = mxq(h, 0, "e4m3").T @ mxq(f64(counts), 0, "e4m3")
    return np.log(pooled)

@@ -1,0 +1,272 @@
+from contextlib import ExitStack
+
+import concourse.mybir as mybir
+from concourse.masks import make_identity
+
+V, K, C, B = 2048, 1024, 1024, 512
+FLOPS = 2 * V * K * C + 2 * V * C * B
+
+F32 = mybir.dt.float32
+BF16 = mybir.dt.bfloat16
+I32 = mybir.dt.int32
+U32 = mybir.dt.uint32
+U8 = mybir.dt.uint8
+FP8X4 = mybir.dt.float8_e4m3fn_x4
+ACT = mybir.ActivationFunctionType
+ALU = mybir.AluOpType
+
+P = 128
+PACK = 4
+PASS = P * PACK
+W = 512
+GROUPS = V // PASS
+KPASSES = K // PASS
+HALVES = C // W
+STEPS = 2 * GROUPS
+DEFER = 2
+UNITS = [[("h", 0, 0)], [("n", 0, 0)], [("h", 0, 1)], [("n", 0, 1)], [("n", 0, 2), ("h", 0, 2)], [("n", 0, 3), ("h", 0, 3)], [], [("h", 1, 0)], [], [("h", 1, 1)], [], [("h", 1, 2)], [], [("h", 1, 3)]]
+LN2 = 0.6931471805599453
+
+
+def tile_kernel_pooled_term_search_s7_kernel(tc, embed, centers, idf, counts, out):
+    nc = tc.nc
+    with ExitStack() as ctx:
+        keep = ctx.enter_context(tc.tile_pool(name="keep", bufs=1))
+        stage = ctx.enter_context(tc.tile_pool(name="stage", bufs=4))
+        psum = ctx.enter_context(tc.psum_pool(name="psum", bufs=1))
+        ctx.enter_context(tc.manual_schedule())
+
+        def bank(i):
+            return psum.tile([P, W], F32, name="bank%d" % i, tag="bank%d" % i)
+
+        def operand(name, width):
+            codes = keep.tile([P, width], U32, name=name + "_codes", align_bytes=64)
+            scales = keep.tile([P, width], U8, name=name + "_scales", align_bytes=64)
+            return codes, scales
+
+        raw = {}
+        mx = {}
+
+        def load_rows(key, rows):
+            raw[key] = keep.tile([P, PACK, W], BF16, name="raw_%s%d%d" % key)
+            nc.sync.dma_start(out=raw[key][:], in_=rows.rearrange("(p j) w -> p j w", j=PACK))
+
+        def load_centers(half, j):
+            load_rows(("c", half, j), centers[j * PASS : (j + 1) * PASS, half * W : (half + 1) * W])
+
+        def load_counts(g):
+            load_rows(("n", 0, g), counts[g * PASS : (g + 1) * PASS, :])
+
+        e_raw = {}
+
+        def load_embed(s):
+            g, pair = divmod(s, 2)
+            e_raw[s] = keep.tile([P, 2, K], BF16, name="e_raw%d" % s)
+            rows = embed[g * PASS : (g + 1) * PASS, :].rearrange("(m t) k -> m t k", t=PACK)
+            nc.sync.dma_start(out=e_raw[s][:], in_=rows[:, 2 * pair : 2 * pair + 2, :])
+
+        grouped = {}
+
+        def interleave(key, copy, c0, c1):
+            if key not in grouped:
+                grouped[key] = stage.tile([P, W, PACK], BF16, name="grouped", align_bytes=64)
+            copy(
+                out=grouped[key][:, c0:c1, :].rearrange("p (c i) t -> p c t i", i=4),
+                in_=raw[key][:, :, c0:c1].rearrange("p t (c i) -> p c t i", i=4),
+            )
+
+        def quantize(key):
+            mx[key] = operand("mx_%s%d%d" % key, W)
+            codes, scales = mx[key]
+            nc.vector.quantize_mx(
+                out=codes[:].bitcast(FP8X4), scales=scales[:], in_=grouped[key][:].rearrange("p w j -> p (w j)")
+            )
+
+        turned = {}
+        e_grouped = {}
+
+        def transpose_embed(s):
+            words = e_raw[s][:].rearrange("p t k -> p (t k)").bitcast(F32)
+            for j in range(KPASSES):
+                turned[s, j] = bank((2 * s + j) % 4)
+                for tt in range(2):
+                    for u in range(2):
+                        w0 = tt * (K // 2) + j * (PASS // 2)
+                        q = 2 * tt + u
+                        nc.tensor.transpose(
+                            turned[s, j][:, q * P : (q + 1) * P], words[:, w0 + u : w0 + PASS // 2 : 2], ident[:]
+                        )
+
+        def copy_turned(s, j, copy):
+            e_grouped[s, j] = stage.tile([P, 2 * P * PACK], BF16, name="e_grouped", align_bytes=64)
+            copy(
+                out=e_grouped[s, j][:].bitcast(F32).rearrange("p (t m u) -> p t m u", t=2, u=2),
+                in_=turned[s, j][:].rearrange("p (t u m) -> p t m u", t=2, u=2),
+            )
+
+        def quantize_embed(s, j):
+            mx["e", s, j] = operand("mx_e%d%d" % (s, j), 2 * P)
+            codes, scales = mx["e", s, j]
+            nc.vector.quantize_mx(out=codes[:].bitcast(FP8X4), scales=scales[:], in_=e_grouped[s, j][:])
+
+        def matmul(acc, stationary, col, moving, n0, n1, first, last):
+            nc.tensor.matmul_mx(
+                out=acc,
+                lhsT=stationary[0][:, col * P : (col + 1) * P].bitcast(FP8X4),
+                lhsT_scale=stationary[1][:, col * P : (col + 1) * P],
+                rhs=moving[0][:, n0:n1].bitcast(FP8X4),
+                rhs_scale=moving[1][:, n0:n1],
+                start=first,
+                stop=last,
+            )
+
+        cos = {}
+
+        def cos_passes(s, half, passes):
+            pair = s % 2
+            for tt in range(2):
+                if 0 in passes:
+                    cos[s, half, tt] = bank(4 + 2 * pair + tt)
+                for j in passes:
+                    matmul(cos[s, half, tt][:], mx["e", s, j], tt, mx["c", half, j], 0, W, j == 0, j == KPASSES - 1)
+
+        def kernel_values(s, half):
+            g, pair = divmod(s, 2)
+            if pair == 0:
+                raw["h", half, g] = keep.tile([P, PACK, W], BF16, name="raw_h%d%d" % (half, g))
+            for tt in range(2):
+                t = 2 * pair + tt
+                col = PACK * g + t
+                nc.scalar.activation(
+                    out=raw["h", half, g][:, t, :], in_=cos[s, half, tt][:], func=ACT.Exp, bias=log_idf[:, col : col + 1]
+                )
+
+        idf_sb = keep.tile([P, GROUPS, PACK], BF16, name="idf_sb")
+        nc.scalar.dma_start(out=idf_sb[:], in_=idf.rearrange("(g p t) -> p g t", p=P, t=PACK))
+        load_embed(0)
+        load_centers(0, 0)
+        load_embed(1)
+        load_embed(2)
+        load_centers(0, 1)
+        load_embed(3)
+        later = [("c", 1, j) for j in range(KPASSES)] + [("n", 0, g) for g in range(GROUPS)]
+        for s in range(4, 4 + len(later)):
+            kind, half, i = later[s - 4]
+            if kind == "c":
+                load_centers(half, i)
+            else:
+                load_counts(i)
+            if s < STEPS:
+                load_embed(s)
+
+        ident = keep.tile([P, P], F32, name="ident")
+        make_identity(nc, ident[:])
+
+        n_cols = GROUPS * PACK
+        idf_f32 = keep.tile([P, n_cols], F32, name="idf_f32")
+        mantissa = keep.tile([P, n_cols], I32, name="mantissa")
+        exponent = keep.tile([P, n_cols], I32, name="exponent")
+        log_exponent = keep.tile([P, n_cols], F32, name="log_exponent")
+        log_mantissa = keep.tile([P, n_cols], F32, name="log_mantissa")
+        log_idf = keep.tile([P, n_cols], F32, name="log_idf")
+        nc.vector.tensor_copy(out=idf_f32[:], in_=idf_sb[:].rearrange("p g t -> p (g t)"))
+        nc.vector.tensor_scalar(
+            out=mantissa[:], in0=idf_f32[:].bitcast(I32), scalar1=0x007FFFFF, scalar2=0x3F800000,
+            op0=ALU.bitwise_and, op1=ALU.bitwise_or,
+        )
+        nc.vector.tensor_scalar(
+            out=exponent[:], in0=idf_f32[:].bitcast(I32), scalar1=23, scalar2=None, op0=ALU.logical_shift_right
+        )
+        nc.scalar.activation(out=log_mantissa[:], in_=mantissa[:].bitcast(F32), func=ACT.Ln)
+        nc.vector.tensor_scalar(
+            out=log_exponent[:], in0=exponent[:], scalar1=-127.0, scalar2=LN2, op0=ALU.add, op1=ALU.mult
+        )
+        nc.vector.tensor_tensor(out=log_idf[:], in0=log_exponent[:], in1=log_mantissa[:], op=ALU.add)
+
+        def turn(s):
+            transpose_embed(s)
+            for j in range(KPASSES):
+                copy_turned(s, j, nc.scalar.copy)
+
+        transpose_embed(0)
+        copy_turned(0, 0, nc.vector.tensor_copy)
+        interleave(("c", 0, 0), nc.vector.tensor_copy, 0, W)
+        copy_turned(0, 1, nc.scalar.copy)
+        quantize_embed(0, 0)
+        quantize(("c", 0, 0))
+        quantize_embed(0, 1)
+        turn(1)
+        cos_passes(0, 0, [0])
+        quantize_embed(1, 0)
+        quantize_embed(1, 1)
+        turn(2)
+        cos_passes(1, 0, [0])
+        interleave(("c", 0, 1), nc.vector.tensor_copy, 0, W)
+        quantize_embed(2, 0)
+        quantize(("c", 0, 1))
+        quantize_embed(2, 1)
+
+        pending = []
+
+        def quantize_pending():
+            if pending:
+                quantize(pending[0])
+                pending.clear()
+
+        def vector_step(unit):
+            interleave(unit, nc.vector.tensor_copy, 0, W)
+            quantize_pending()
+            pending.append(unit)
+
+        turn(3)
+        cos_passes(0, 0, [1])
+        cos_passes(1, 0, [1])
+        kernel_values(0, 0)
+        kernel_values(1, 0)
+        vector_step(("c", 1, 0))
+        quantize_embed(3, 0)
+        quantize_pending()
+        quantize_embed(3, 1)
+        vector_step(("c", 1, 1))
+        units = UNITS
+        for s in range(2, STEPS):
+            if s + 2 < STEPS:
+                turn(s + 2)
+                quantize_embed(s + 2, 0)
+                quantize_pending()
+                quantize_embed(s + 2, 1)
+            cos_passes(s, 0, [0, 1])
+            kernel_values(s, 0)
+            for unit in units[s - 2]:
+                vector_step(unit)
+
+        for s in range(STEPS):
+            cos_passes(s, 1, [0, 1])
+            kernel_values(s, 1)
+            for unit in units[STEPS - 2 + s]:
+                vector_step(unit)
+        quantize_pending()
+
+        pooled = {}
+
+        def pool_passes(i, n0, n1, groups, b):
+            half, col = divmod(i, W // P)
+            if 0 in groups:
+                pooled[i, n0] = bank(b)
+            for g in groups:
+                matmul(pooled[i, n0][:, : n1 - n0], mx["h", half, g], col, mx["n", 0, g], n0, n1, g == 0, g == GROUPS - 1)
+            if GROUPS - 1 in groups:
+                result = keep.tile([P, n1 - n0], F32, name="result%d_%d" % (i, n0))
+                nc.scalar.activation(out=result[:], in_=pooled[i, n0][:, : n1 - n0], func=ACT.Ln)
+                nc.sync.dma_start(out=out[i * P : (i + 1) * P, n0:n1], in_=result[:])
+
+        for i in range(4):
+            pool_passes(i, 0, B, [0, 1, 2, 3], i)
+        for i in range(4, 4 + DEFER):
+            pool_passes(i, 0, B, [0, 1, 2], i)
+        for i in range(4, 4 + DEFER):
+            pool_passes(i, 0, B, [3], i)
+        for i in range(4 + DEFER, 7):
+            pool_passes(i, 0, B, [0, 1, 2, 3], i)
+        pool_passes(7, 0, B // 2, [0, 1, 2, 3], 7)
+        pool_passes(7, B // 2, B, [0, 1, 2, 3], 0)

@@ -24,6 +24,10 @@ KPASSES = K // PASS
 HALVES = C // W
 STEPS = 2 * GROUPS
 DEFER = 2
+WARM_A = 9
+WARM_B = 5
+RUN = 1
+LAST = 256
 UNITS = [[("h", 0, 0)], [("n", 0, 0)], [("h", 0, 1)], [("n", 0, 1)], [("n", 0, 2), ("h", 0, 2)], [("n", 0, 3), ("h", 0, 3)], [], [("h", 1, 0)], [], [("h", 1, 1)], [], [("h", 1, 2)], [], [("h", 1, 3)]]
 LN2 = 0.6931471805599453
 
@@ -126,7 +130,7 @@ def tile_kernel_pooled_term_search_s7_kernel(tc, embed, centers, idf, counts, ou
             pair = s % 2
             for tt in range(2):
                 if 0 in passes:
-                    cos[s, half, tt] = bank(4 + 2 * pair + tt)
+                    cos[s, half, tt] = bank(4 + 2 * pair + tt if half == 0 else (2 * s + tt) % 8)
                 for j in passes:
                     matmul(cos[s, half, tt][:], mx["e", s, j], tt, mx["c", half, j], 0, W, j == 0, j == KPASSES - 1)
 
@@ -162,6 +166,11 @@ def tile_kernel_pooled_term_search_s7_kernel(tc, embed, centers, idf, counts, ou
         ident = keep.tile([P, P], F32, name="ident")
         make_identity(nc, ident[:])
 
+        filler = keep.tile([P, 2 * P * PACK], BF16, name="filler", align_bytes=64)
+        nc.vector.memset(filler[:], 0.0)
+        warm_mx = operand("warm_mx", 2 * P)
+        nc.vector.quantize_mx(out=warm_mx[0][:].bitcast(FP8X4), scales=warm_mx[1][:], in_=filler[:])
+
         n_cols = GROUPS * PACK
         idf_f32 = keep.tile([P, n_cols], F32, name="idf_f32")
         mantissa = keep.tile([P, n_cols], I32, name="mantissa")
@@ -169,6 +178,7 @@ def tile_kernel_pooled_term_search_s7_kernel(tc, embed, centers, idf, counts, ou
         log_exponent = keep.tile([P, n_cols], F32, name="log_exponent")
         log_mantissa = keep.tile([P, n_cols], F32, name="log_mantissa")
         log_idf = keep.tile([P, n_cols], F32, name="log_idf")
+        warm = keep.tile([P, 1], F32, name="warm")
         nc.vector.tensor_copy(out=idf_f32[:], in_=idf_sb[:].rearrange("p g t -> p (g t)"))
         nc.vector.tensor_scalar(
             out=mantissa[:], in0=idf_f32[:].bitcast(I32), scalar1=0x007FFFFF, scalar2=0x3F800000,
@@ -178,6 +188,7 @@ def tile_kernel_pooled_term_search_s7_kernel(tc, embed, centers, idf, counts, ou
             out=exponent[:], in0=idf_f32[:].bitcast(I32), scalar1=23, scalar2=None, op0=ALU.logical_shift_right
         )
         nc.scalar.activation(out=log_mantissa[:], in_=mantissa[:].bitcast(F32), func=ACT.Ln)
+        nc.scalar.activation(out=warm[:], in_=log_mantissa[:, 0:1], func=ACT.Exp)
         nc.vector.tensor_scalar(
             out=log_exponent[:], in0=exponent[:], scalar1=-127.0, scalar2=LN2, op0=ALU.add, op1=ALU.mult
         )
@@ -188,10 +199,16 @@ def tile_kernel_pooled_term_search_s7_kernel(tc, embed, centers, idf, counts, ou
             for j in range(KPASSES):
                 copy_turned(s, j, nc.scalar.copy)
 
-        transpose_embed(0)
-        copy_turned(0, 0, nc.vector.tensor_copy)
+        warm_bank = bank(7)
+
+        def warm_tensor(n):
+            for i in range(n):
+                matmul(warm_bank[:, : 2 * P], warm_mx, 0, warm_mx, 0, 2 * P, True, True)
+
+        warm_tensor(WARM_A)
+        turn(0)
+        warm_tensor(WARM_B)
         interleave(("c", 0, 0), nc.vector.tensor_copy, 0, W)
-        copy_turned(0, 1, nc.scalar.copy)
         quantize_embed(0, 0)
         quantize(("c", 0, 0))
         quantize_embed(0, 1)
@@ -229,16 +246,21 @@ def tile_kernel_pooled_term_search_s7_kernel(tc, embed, centers, idf, counts, ou
         quantize_embed(3, 1)
         vector_step(("c", 1, 1))
         units = UNITS
-        for s in range(2, STEPS):
-            if s + 2 < STEPS:
-                turn(s + 2)
-                quantize_embed(s + 2, 0)
-                quantize_pending()
-                quantize_embed(s + 2, 1)
-            cos_passes(s, 0, [0, 1])
-            kernel_values(s, 0)
-            for unit in units[s - 2]:
-                vector_step(unit)
+        for s0 in range(2, STEPS, RUN):
+            run = range(s0, s0 + RUN)
+            for s in run:
+                if s + 2 < STEPS:
+                    turn(s + 2)
+            for s in run:
+                cos_passes(s, 0, [0, 1])
+                kernel_values(s, 0)
+            for s in run:
+                if s + 2 < STEPS:
+                    quantize_embed(s + 2, 0)
+                    quantize_pending()
+                    quantize_embed(s + 2, 1)
+                for unit in units[s - 2]:
+                    vector_step(unit)
 
         for s in range(STEPS):
             cos_passes(s, 1, [0, 1])
@@ -258,7 +280,8 @@ def tile_kernel_pooled_term_search_s7_kernel(tc, embed, centers, idf, counts, ou
             if GROUPS - 1 in groups:
                 result = keep.tile([P, n1 - n0], F32, name="result%d_%d" % (i, n0))
                 nc.scalar.activation(out=result[:], in_=pooled[i, n0][:, : n1 - n0], func=ACT.Ln)
-                nc.sync.dma_start(out=out[i * P : (i + 1) * P, n0:n1], in_=result[:])
+                queue = nc.scalar if (i, n1) == (C // P - 1, B) else nc.sync
+                queue.dma_start(out=out[i * P : (i + 1) * P, n0:n1], in_=result[:])
 
         for i in range(4):
             pool_passes(i, 0, B, [0, 1, 2, 3], i)
@@ -269,4 +292,5 @@ def tile_kernel_pooled_term_search_s7_kernel(tc, embed, centers, idf, counts, ou
         for i in range(4 + DEFER, 7):
             pool_passes(i, 0, B, [0, 1, 2, 3], i)
         pool_passes(7, 0, B // 2, [0, 1, 2, 3], 7)
-        pool_passes(7, B // 2, B, [0, 1, 2, 3], 0)
+        for b, n0 in enumerate(range(B // 2, B, LAST)):
+            pool_passes(7, n0, n0 + LAST, [0, 1, 2, 3], b)

@@ -23,12 +23,18 @@ GROUPS = V // PASS
 KPASSES = K // PASS
 HALVES = C // W
 STEPS = 2 * GROUPS
-DEFER = 2
-WARM_A = 9
-WARM_B = 5
-RUN = 1
+DEFER = 0
+WARM_A = 14
+WARM_B = 8
+LAG = 8
+QLAG = 0
+VCOPY = [(3, 0), (4, 0)]
+PRE = {2: [("h", 0, 0)]}
+DEFER0 = 2
+NSTART = 3
+LOADS = [("e", 0), ("c", 0, 0), ("e", 1), ("e", 2), ("c", 0, 1), ("e", 3), ("e", 4), ("c", 1, 0), ("e", 5), ("c", 1, 1), ("e", 6), ("e", 7), ("n", 0), ("n", 1), ("n", 2), ("n", 3)]
 LAST = 256
-UNITS = [[("h", 0, 0)], [("n", 0, 0)], [("h", 0, 1)], [("n", 0, 1)], [("n", 0, 2), ("h", 0, 2)], [("n", 0, 3), ("h", 0, 3)], [], [("h", 1, 0)], [], [("h", 1, 1)], [], [("h", 1, 2)], [], [("h", 1, 3)]]
+UNITS = [[], [("c", 1, 0)], [("c", 1, 1)], [("h", 0, 1)], [], [("n", 0, 0)], [("h", 0, 2), ("n", 0, 1)], [("n", 0, 2), ("h", 0, 3)], [("n", 0, 3)], [("h", 1, 0)], [], [("h", 1, 1)], [], [], [], [("h", 1, g, q) for q in range(4) for g in (2, 3)]]
 LN2 = 0.6931471805599453
 
 
@@ -52,7 +58,7 @@ def tile_kernel_pooled_term_search_s7_kernel(tc, embed, centers, idf, counts, ou
         mx = {}
 
         def load_rows(key, rows):
-            raw[key] = keep.tile([P, PACK, W], BF16, name="raw_%s%d%d" % key)
+            raw[key] = keep.tile([P, PACK, W], BF16, name="raw_%s%d%d" % key, align_bytes=256)
             nc.sync.dma_start(out=raw[key][:], in_=rows.rearrange("(p j) w -> p j w", j=PACK))
 
         def load_centers(half, j):
@@ -65,25 +71,29 @@ def tile_kernel_pooled_term_search_s7_kernel(tc, embed, centers, idf, counts, ou
 
         def load_embed(s):
             g, pair = divmod(s, 2)
-            e_raw[s] = keep.tile([P, 2, K], BF16, name="e_raw%d" % s)
+            e_raw[s] = keep.tile([P, 2, K], BF16, name="e_raw%d" % s, align_bytes=256)
             rows = embed[g * PASS : (g + 1) * PASS, :].rearrange("(m t) k -> m t k", t=PACK)
             nc.sync.dma_start(out=e_raw[s][:], in_=rows[:, 2 * pair : 2 * pair + 2, :])
 
         grouped = {}
 
-        def interleave(key, copy, c0, c1):
-            if key not in grouped:
-                grouped[key] = stage.tile([P, W, PACK], BF16, name="grouped", align_bytes=64)
-            copy(
-                out=grouped[key][:, c0:c1, :].rearrange("p (c i) t -> p c t i", i=4),
+        def interleave(unit):
+            key, c0, c1 = unit
+            grouped[unit] = stage.tile([P, c1 - c0, PACK], BF16, name="grouped", align_bytes=64)
+            nc.vector.tensor_copy(
+                out=grouped[unit][:].rearrange("p (c i) t -> p c t i", i=4),
                 in_=raw[key][:, :, c0:c1].rearrange("p t (c i) -> p c t i", i=4),
             )
 
-        def quantize(key):
-            mx[key] = operand("mx_%s%d%d" % key, W)
+        def quantize(unit):
+            key, c0, c1 = unit
+            if key not in mx:
+                mx[key] = operand("mx_%s%d%d" % key, W)
             codes, scales = mx[key]
             nc.vector.quantize_mx(
-                out=codes[:].bitcast(FP8X4), scales=scales[:], in_=grouped[key][:].rearrange("p w j -> p (w j)")
+                out=codes[:, c0:c1].bitcast(FP8X4),
+                scales=scales[:, c0:c1],
+                in_=grouped[unit][:].rearrange("p w j -> p (w j)"),
             )
 
         turned = {}
@@ -125,12 +135,14 @@ def tile_kernel_pooled_term_search_s7_kernel(tc, embed, centers, idf, counts, ou
             )
 
         cos = {}
+        n_early = 2 * (STEPS - 2 + max(0, STEPS - 2 - LAG))
+        cos_banks = [4 + n % 4 for n in range(n_early)] + [(n - 4 * STEPS) % 8 for n in range(n_early, 4 * STEPS)]
 
         def cos_passes(s, half, passes):
             pair = s % 2
             for tt in range(2):
                 if 0 in passes:
-                    cos[s, half, tt] = bank(4 + 2 * pair + tt if half == 0 else (2 * s + tt) % 8)
+                    cos[s, half, tt] = bank(cos_banks[len(cos)])
                 for j in passes:
                     matmul(cos[s, half, tt][:], mx["e", s, j], tt, mx["c", half, j], 0, W, j == 0, j == KPASSES - 1)
 
@@ -147,28 +159,20 @@ def tile_kernel_pooled_term_search_s7_kernel(tc, embed, centers, idf, counts, ou
 
         idf_sb = keep.tile([P, GROUPS, PACK], BF16, name="idf_sb")
         nc.scalar.dma_start(out=idf_sb[:], in_=idf.rearrange("(g p t) -> p g t", p=P, t=PACK))
-        load_embed(0)
-        load_centers(0, 0)
-        load_embed(1)
-        load_embed(2)
-        load_centers(0, 1)
-        load_embed(3)
-        later = [("c", 1, j) for j in range(KPASSES)] + [("n", 0, g) for g in range(GROUPS)]
-        for s in range(4, 4 + len(later)):
-            kind, half, i = later[s - 4]
-            if kind == "c":
-                load_centers(half, i)
+        for key in LOADS:
+            if key[0] == "e":
+                load_embed(key[1])
+            elif key[0] == "c":
+                load_centers(key[1], key[2])
             else:
-                load_counts(i)
-            if s < STEPS:
-                load_embed(s)
+                load_counts(key[1])
 
         ident = keep.tile([P, P], F32, name="ident")
         make_identity(nc, ident[:])
 
-        filler = keep.tile([P, 2 * P * PACK], BF16, name="filler", align_bytes=64)
-        nc.vector.memset(filler[:], 0.0)
-        warm_mx = operand("warm_mx", 2 * P)
+        filler = keep.tile([P, P * PACK], BF16, name="filler", align_bytes=64)
+        nc.vector.memset(filler[:].bitcast(I32), 0)
+        warm_mx = operand("warm_mx", P)
         nc.vector.quantize_mx(out=warm_mx[0][:].bitcast(FP8X4), scales=warm_mx[1][:], in_=filler[:])
 
         n_cols = GROUPS * PACK
@@ -189,38 +193,40 @@ def tile_kernel_pooled_term_search_s7_kernel(tc, embed, centers, idf, counts, ou
         )
         nc.scalar.activation(out=log_mantissa[:], in_=mantissa[:].bitcast(F32), func=ACT.Ln)
         nc.scalar.activation(out=warm[:], in_=log_mantissa[:, 0:1], func=ACT.Exp)
-        nc.vector.tensor_scalar(
-            out=log_exponent[:], in0=exponent[:], scalar1=-127.0, scalar2=LN2, op0=ALU.add, op1=ALU.mult
-        )
-        nc.vector.tensor_tensor(out=log_idf[:], in0=log_exponent[:], in1=log_mantissa[:], op=ALU.add)
 
         def turn(s):
             transpose_embed(s)
             for j in range(KPASSES):
-                copy_turned(s, j, nc.scalar.copy)
+                copy_turned(s, j, nc.vector.tensor_copy if (s, j) in VCOPY else nc.scalar.copy)
 
         warm_bank = bank(7)
 
         def warm_tensor(n):
             for i in range(n):
-                matmul(warm_bank[:, : 2 * P], warm_mx, 0, warm_mx, 0, 2 * P, True, True)
+                matmul(warm_bank[:, :P], warm_mx, 0, warm_mx, 0, P, True, True)
 
         warm_tensor(WARM_A)
-        turn(0)
+        transpose_embed(0)
         warm_tensor(WARM_B)
-        interleave(("c", 0, 0), nc.vector.tensor_copy, 0, W)
+        copy_turned(0, 0, nc.vector.tensor_copy)
+        interleave((("c", 0, 0), 0, W))
+        copy_turned(0, 1, nc.scalar.copy)
         quantize_embed(0, 0)
-        quantize(("c", 0, 0))
+        quantize((("c", 0, 0), 0, W))
         quantize_embed(0, 1)
         turn(1)
         cos_passes(0, 0, [0])
         quantize_embed(1, 0)
         quantize_embed(1, 1)
+        nc.vector.tensor_scalar(
+            out=log_exponent[:], in0=exponent[:], scalar1=-127.0, scalar2=LN2, op0=ALU.add, op1=ALU.mult
+        )
+        nc.vector.tensor_tensor(out=log_idf[:], in0=log_exponent[:], in1=log_mantissa[:], op=ALU.add)
         turn(2)
         cos_passes(1, 0, [0])
-        interleave(("c", 0, 1), nc.vector.tensor_copy, 0, W)
+        interleave((("c", 0, 1), 0, W))
         quantize_embed(2, 0)
-        quantize(("c", 0, 1))
+        quantize((("c", 0, 1), 0, W))
         quantize_embed(2, 1)
 
         pending = []
@@ -231,42 +237,41 @@ def tile_kernel_pooled_term_search_s7_kernel(tc, embed, centers, idf, counts, ou
                 pending.clear()
 
         def vector_step(unit):
-            interleave(unit, nc.vector.tensor_copy, 0, W)
+            interleave(unit)
             quantize_pending()
             pending.append(unit)
+
+        def vector_units(keys):
+            for key in keys:
+                if len(key) == 3:
+                    vector_step((key, 0, W))
+                else:
+                    vector_step((key[:3], key[3] * P, (key[3] + 1) * P))
 
         turn(3)
         cos_passes(0, 0, [1])
         cos_passes(1, 0, [1])
         kernel_values(0, 0)
         kernel_values(1, 0)
-        vector_step(("c", 1, 0))
-        quantize_embed(3, 0)
-        quantize_pending()
-        quantize_embed(3, 1)
-        vector_step(("c", 1, 1))
-        units = UNITS
-        for s0 in range(2, STEPS, RUN):
-            run = range(s0, s0 + RUN)
-            for s in run:
-                if s + 2 < STEPS:
-                    turn(s + 2)
-            for s in run:
-                cos_passes(s, 0, [0, 1])
-                kernel_values(s, 0)
-            for s in run:
-                if s + 2 < STEPS:
-                    quantize_embed(s + 2, 0)
-                    quantize_pending()
-                    quantize_embed(s + 2, 1)
-                for unit in units[s - 2]:
-                    vector_step(unit)
-
-        for s in range(STEPS):
-            cos_passes(s, 1, [0, 1])
-            kernel_values(s, 1)
-            for unit in units[STEPS - 2 + s]:
-                vector_step(unit)
+        vector_units(UNITS[0])
+        if QLAG == 0:
+            quantize_embed(3, 0)
+            quantize_pending()
+            quantize_embed(3, 1)
+        vector_units(UNITS[1])
+        for r in range(2, STEPS + LAG):
+            if r + 2 < STEPS:
+                turn(r + 2)
+            vector_units(PRE.get(r, []))
+            if r + 2 - QLAG < STEPS:
+                quantize_embed(r + 2 - QLAG, 0)
+                quantize_pending()
+                quantize_embed(r + 2 - QLAG, 1)
+            for half, s in ((0, r), (1, r - LAG)):
+                if 0 <= s < STEPS:
+                    cos_passes(s, half, [0, 1])
+                    kernel_values(s, half)
+            vector_units(UNITS[r])
         quantize_pending()
 
         pooled = {}
@@ -278,12 +283,16 @@ def tile_kernel_pooled_term_search_s7_kernel(tc, embed, centers, idf, counts, ou
             for g in groups:
                 matmul(pooled[i, n0][:, : n1 - n0], mx["h", half, g], col, mx["n", 0, g], n0, n1, g == 0, g == GROUPS - 1)
             if GROUPS - 1 in groups:
-                result = keep.tile([P, n1 - n0], F32, name="result%d_%d" % (i, n0))
+                result = keep.tile([P, n1 - n0], F32, name="result%d_%d" % (i, n0), align_bytes=256)
                 nc.scalar.activation(out=result[:], in_=pooled[i, n0][:, : n1 - n0], func=ACT.Ln)
                 queue = nc.scalar if (i, n1) == (C // P - 1, B) else nc.sync
                 queue.dma_start(out=out[i * P : (i + 1) * P, n0:n1], in_=result[:])
 
-        for i in range(4):
+        for i in range(DEFER0):
+            pool_passes(i, 0, B, [0, 1, 2], i)
+        for i in range(DEFER0):
+            pool_passes(i, 0, B, [3], i)
+        for i in range(DEFER0, 4):
             pool_passes(i, 0, B, [0, 1, 2, 3], i)
         for i in range(4, 4 + DEFER):
             pool_passes(i, 0, B, [0, 1, 2], i)

from contextlib import ExitStack

import concourse.mybir as mybir
from concourse.masks import make_identity

V, K, C, B = 2048, 1024, 1024, 512
FLOPS = 2 * V * K * C + 2 * V * C * B

F32 = mybir.dt.float32
BF16 = mybir.dt.bfloat16
I32 = mybir.dt.int32
U32 = mybir.dt.uint32
U8 = mybir.dt.uint8
FP8X4 = mybir.dt.float8_e4m3fn_x4
ACT = mybir.ActivationFunctionType
ALU = mybir.AluOpType

P = 128
PACK = 4
PASS = P * PACK
W = 512
GROUPS = V // PASS
KPASSES = K // PASS
HALVES = C // W
STEPS = 2 * GROUPS
DEFER = 0
WARM_A = 14
WARM_B = 8
LAG = 8
QLAG = 0
VCOPY = [(3, 0), (4, 0)]
PRE = {2: [("h", 0, 0)]}
DEFER0 = 2
NSTART = 3
LOADS = [("e", 0), ("c", 0, 0), ("e", 1), ("e", 2), ("c", 0, 1), ("e", 3), ("e", 4), ("c", 1, 0), ("e", 5), ("c", 1, 1), ("e", 6), ("e", 7), ("n", 0), ("n", 1), ("n", 2), ("n", 3)]
LAST = 256
UNITS = [[], [("c", 1, 0)], [("c", 1, 1)], [("h", 0, 1)], [], [("n", 0, 0)], [("h", 0, 2), ("n", 0, 1)], [("n", 0, 2), ("h", 0, 3)], [("n", 0, 3)], [("h", 1, 0)], [], [("h", 1, 1)], [], [], [], [("h", 1, g, q) for q in range(4) for g in (2, 3)]]
LN2 = 0.6931471805599453


def tile_kernel_pooled_term_search_s7_kernel(tc, embed, centers, idf, counts, out):
    nc = tc.nc
    with ExitStack() as ctx:
        keep = ctx.enter_context(tc.tile_pool(name="keep", bufs=1))
        stage = ctx.enter_context(tc.tile_pool(name="stage", bufs=4))
        psum = ctx.enter_context(tc.psum_pool(name="psum", bufs=1))
        ctx.enter_context(tc.manual_schedule())

        def bank(i):
            return psum.tile([P, W], F32, name="bank%d" % i, tag="bank%d" % i)

        def operand(name, width):
            codes = keep.tile([P, width], U32, name=name + "_codes", align_bytes=64)
            scales = keep.tile([P, width], U8, name=name + "_scales", align_bytes=64)
            return codes, scales

        raw = {}
        mx = {}

        def load_rows(key, rows):
            raw[key] = keep.tile([P, PACK, W], BF16, name="raw_%s%d%d" % key, align_bytes=256)
            nc.sync.dma_start(out=raw[key][:], in_=rows.rearrange("(p j) w -> p j w", j=PACK))

        def load_centers(half, j):
            load_rows(("c", half, j), centers[j * PASS : (j + 1) * PASS, half * W : (half + 1) * W])

        def load_counts(g):
            load_rows(("n", 0, g), counts[g * PASS : (g + 1) * PASS, :])

        e_raw = {}

        def load_embed(s):
            g, pair = divmod(s, 2)
            e_raw[s] = keep.tile([P, 2, K], BF16, name="e_raw%d" % s, align_bytes=256)
            rows = embed[g * PASS : (g + 1) * PASS, :].rearrange("(m t) k -> m t k", t=PACK)
            nc.sync.dma_start(out=e_raw[s][:], in_=rows[:, 2 * pair : 2 * pair + 2, :])

        grouped = {}

        def interleave(unit):
            key, c0, c1 = unit
            grouped[unit] = stage.tile([P, c1 - c0, PACK], BF16, name="grouped", align_bytes=64)
            nc.vector.tensor_copy(
                out=grouped[unit][:].rearrange("p (c i) t -> p c t i", i=4),
                in_=raw[key][:, :, c0:c1].rearrange("p t (c i) -> p c t i", i=4),
            )

        def quantize(unit):
            key, c0, c1 = unit
            if key not in mx:
                mx[key] = operand("mx_%s%d%d" % key, W)
            codes, scales = mx[key]
            nc.vector.quantize_mx(
                out=codes[:, c0:c1].bitcast(FP8X4),
                scales=scales[:, c0:c1],
                in_=grouped[unit][:].rearrange("p w j -> p (w j)"),
            )

        turned = {}
        e_grouped = {}

        def transpose_embed(s):
            words = e_raw[s][:].rearrange("p t k -> p (t k)").bitcast(F32)
            for j in range(KPASSES):
                turned[s, j] = bank((2 * s + j) % 4)
                for tt in range(2):
                    for u in range(2):
                        w0 = tt * (K // 2) + j * (PASS // 2)
                        q = 2 * tt + u
                        nc.tensor.transpose(
                            turned[s, j][:, q * P : (q + 1) * P], words[:, w0 + u : w0 + PASS // 2 : 2], ident[:]
                        )

        def copy_turned(s, j, copy):
            e_grouped[s, j] = stage.tile([P, 2 * P * PACK], BF16, name="e_grouped", align_bytes=64)
            copy(
                out=e_grouped[s, j][:].bitcast(F32).rearrange("p (t m u) -> p t m u", t=2, u=2),
                in_=turned[s, j][:].rearrange("p (t u m) -> p t m u", t=2, u=2),
            )

        def quantize_embed(s, j):
            mx["e", s, j] = operand("mx_e%d%d" % (s, j), 2 * P)
            codes, scales = mx["e", s, j]
            nc.vector.quantize_mx(out=codes[:].bitcast(FP8X4), scales=scales[:], in_=e_grouped[s, j][:])

        def matmul(acc, stationary, col, moving, n0, n1, first, last):
            nc.tensor.matmul_mx(
                out=acc,
                lhsT=stationary[0][:, col * P : (col + 1) * P].bitcast(FP8X4),
                lhsT_scale=stationary[1][:, col * P : (col + 1) * P],
                rhs=moving[0][:, n0:n1].bitcast(FP8X4),
                rhs_scale=moving[1][:, n0:n1],
                start=first,
                stop=last,
            )

        cos = {}
        n_early = 2 * (STEPS - 2 + max(0, STEPS - 2 - LAG))
        cos_banks = [4 + n % 4 for n in range(n_early)] + [(n - 4 * STEPS) % 8 for n in range(n_early, 4 * STEPS)]

        def cos_passes(s, half, passes):
            pair = s % 2
            for tt in range(2):
                if 0 in passes:
                    cos[s, half, tt] = bank(cos_banks[len(cos)])
                for j in passes:
                    matmul(cos[s, half, tt][:], mx["e", s, j], tt, mx["c", half, j], 0, W, j == 0, j == KPASSES - 1)

        def kernel_values(s, half):
            g, pair = divmod(s, 2)
            if pair == 0:
                raw["h", half, g] = keep.tile([P, PACK, W], BF16, name="raw_h%d%d" % (half, g))
            for tt in range(2):
                t = 2 * pair + tt
                col = PACK * g + t
                nc.scalar.activation(
                    out=raw["h", half, g][:, t, :], in_=cos[s, half, tt][:], func=ACT.Exp, bias=log_idf[:, col : col + 1]
                )

        idf_sb = keep.tile([P, GROUPS, PACK], BF16, name="idf_sb")
        nc.scalar.dma_start(out=idf_sb[:], in_=idf.rearrange("(g p t) -> p g t", p=P, t=PACK))
        for key in LOADS:
            if key[0] == "e":
                load_embed(key[1])
            elif key[0] == "c":
                load_centers(key[1], key[2])
            else:
                load_counts(key[1])

        ident = keep.tile([P, P], F32, name="ident")
        make_identity(nc, ident[:])

        filler = keep.tile([P, P * PACK], BF16, name="filler", align_bytes=64)
        nc.vector.memset(filler[:].bitcast(I32), 0)
        warm_mx = operand("warm_mx", P)
        nc.vector.quantize_mx(out=warm_mx[0][:].bitcast(FP8X4), scales=warm_mx[1][:], in_=filler[:])

        n_cols = GROUPS * PACK
        idf_f32 = keep.tile([P, n_cols], F32, name="idf_f32")
        mantissa = keep.tile([P, n_cols], I32, name="mantissa")
        exponent = keep.tile([P, n_cols], I32, name="exponent")
        log_exponent = keep.tile([P, n_cols], F32, name="log_exponent")
        log_mantissa = keep.tile([P, n_cols], F32, name="log_mantissa")
        log_idf = keep.tile([P, n_cols], F32, name="log_idf")
        warm = keep.tile([P, 1], F32, name="warm")
        nc.vector.tensor_copy(out=idf_f32[:], in_=idf_sb[:].rearrange("p g t -> p (g t)"))
        nc.vector.tensor_scalar(
            out=mantissa[:], in0=idf_f32[:].bitcast(I32), scalar1=0x007FFFFF, scalar2=0x3F800000,
            op0=ALU.bitwise_and, op1=ALU.bitwise_or,
        )
        nc.vector.tensor_scalar(
            out=exponent[:], in0=idf_f32[:].bitcast(I32), scalar1=23, scalar2=None, op0=ALU.logical_shift_right
        )
        nc.scalar.activation(out=log_mantissa[:], in_=mantissa[:].bitcast(F32), func=ACT.Ln)
        nc.scalar.activation(out=warm[:], in_=log_mantissa[:, 0:1], func=ACT.Exp)

        def turn(s):
            transpose_embed(s)
            for j in range(KPASSES):
                copy_turned(s, j, nc.vector.tensor_copy if (s, j) in VCOPY else nc.scalar.copy)

        warm_bank = bank(7)

        def warm_tensor(n):
            for i in range(n):
                matmul(warm_bank[:, :P], warm_mx, 0, warm_mx, 0, P, True, True)

        warm_tensor(WARM_A)
        transpose_embed(0)
        warm_tensor(WARM_B)
        copy_turned(0, 0, nc.vector.tensor_copy)
        interleave((("c", 0, 0), 0, W))
        copy_turned(0, 1, nc.scalar.copy)
        quantize_embed(0, 0)
        quantize((("c", 0, 0), 0, W))
        quantize_embed(0, 1)
        turn(1)
        cos_passes(0, 0, [0])
        quantize_embed(1, 0)
        quantize_embed(1, 1)
        nc.vector.tensor_scalar(
            out=log_exponent[:], in0=exponent[:], scalar1=-127.0, scalar2=LN2, op0=ALU.add, op1=ALU.mult
        )
        nc.vector.tensor_tensor(out=log_idf[:], in0=log_exponent[:], in1=log_mantissa[:], op=ALU.add)
        turn(2)
        cos_passes(1, 0, [0])
        interleave((("c", 0, 1), 0, W))
        quantize_embed(2, 0)
        quantize((("c", 0, 1), 0, W))
        quantize_embed(2, 1)

        pending = []

        def quantize_pending():
            if pending:
                quantize(pending[0])
                pending.clear()

        def vector_step(unit):
            interleave(unit)
            quantize_pending()
            pending.append(unit)

        def vector_units(keys):
            for key in keys:
                if len(key) == 3:
                    vector_step((key, 0, W))
                else:
                    vector_step((key[:3], key[3] * P, (key[3] + 1) * P))

        turn(3)
        cos_passes(0, 0, [1])
        cos_passes(1, 0, [1])
        kernel_values(0, 0)
        kernel_values(1, 0)
        vector_units(UNITS[0])
        if QLAG == 0:
            quantize_embed(3, 0)
            quantize_pending()
            quantize_embed(3, 1)
        vector_units(UNITS[1])
        for r in range(2, STEPS + LAG):
            if r + 2 < STEPS:
                turn(r + 2)
            vector_units(PRE.get(r, []))
            if r + 2 - QLAG < STEPS:
                quantize_embed(r + 2 - QLAG, 0)
                quantize_pending()
                quantize_embed(r + 2 - QLAG, 1)
            for half, s in ((0, r), (1, r - LAG)):
                if 0 <= s < STEPS:
                    cos_passes(s, half, [0, 1])
                    kernel_values(s, half)
            vector_units(UNITS[r])
        quantize_pending()

        pooled = {}

        def pool_passes(i, n0, n1, groups, b):
            half, col = divmod(i, W // P)
            if 0 in groups:
                pooled[i, n0] = bank(b)
            for g in groups:
                matmul(pooled[i, n0][:, : n1 - n0], mx["h", half, g], col, mx["n", 0, g], n0, n1, g == 0, g == GROUPS - 1)
            if GROUPS - 1 in groups:
                result = keep.tile([P, n1 - n0], F32, name="result%d_%d" % (i, n0), align_bytes=256)
                nc.scalar.activation(out=result[:], in_=pooled[i, n0][:, : n1 - n0], func=ACT.Ln)
                queue = nc.scalar if (i, n1) == (C // P - 1, B) else nc.sync
                queue.dma_start(out=out[i * P : (i + 1) * P, n0:n1], in_=result[:])

        for i in range(DEFER0):
            pool_passes(i, 0, B, [0, 1, 2], i)
        for i in range(DEFER0):
            pool_passes(i, 0, B, [3], i)
        for i in range(DEFER0, 4):
            pool_passes(i, 0, B, [0, 1, 2, 3], i)
        for i in range(4, 4 + DEFER):
            pool_passes(i, 0, B, [0, 1, 2], i)
        for i in range(4, 4 + DEFER):
            pool_passes(i, 0, B, [3], i)
        for i in range(4 + DEFER, 7):
            pool_passes(i, 0, B, [0, 1, 2, 3], i)
        pool_passes(7, 0, B // 2, [0, 1, 2, 3], 7)
        for b, n0 in enumerate(range(B // 2, B, LAST)):
            pool_passes(7, n0, n0 + LAST, [0, 1, 2, 3], b)
